import numpy as np
import ml_dtypes


def mxq(x, axis, fmt="e4m3"):
    dtype, down = {"e4m3": (ml_dtypes.float8_e4m3fn, 7), "e5m2": (ml_dtypes.float8_e5m2, 14)}[fmt]
    v = np.moveaxis(np.asarray(x, np.float32).astype(ml_dtypes.bfloat16).astype(np.float64), axis, -1)
    blocks = v.reshape(v.shape[:-1] + (-1, 32))
    amax = np.abs(blocks).max(-1, keepdims=True)
    byte = np.maximum(np.where(amax > 0, np.frexp(amax)[1] - 1 + 127, 0) - down, 1)
    scale = np.exp2(byte - 127.0)
    codes = (blocks / scale).astype(np.float32).astype(dtype).astype(np.float64)
    return np.moveaxis((codes * scale).reshape(v.shape), -1, axis)


WIDE = False


def mx_kscale(k):
    if not WIDE:
        return np.ones(k)
    levels = np.array([10, -10, 5, -5, 0])
    if k % 512:
        return np.exp2(np.random.permutation(np.resize(levels, k // 32))).repeat(32)
    a = np.empty((k // 512, 16))
    for p in range(k // 512):
        a[p, :8] = np.random.permutation(np.resize(levels, 8))
        for g in range(8):
            far = levels[np.abs(levels - a[p, g]) >= 10]
            a[p, g + 8] = far[np.random.randint(len(far))]
    return np.exp2(a.ravel()).repeat(32)


BF16 = ml_dtypes.bfloat16


def bf(x):
    return np.asarray(x, np.float32).astype(BF16)


def f64(x):
    return np.asarray(x).astype(np.float64)


E2M1 = np.array([0.0, 0.5, 1.0, 1.5, 2.0, 3.0, 4.0, 6.0, -0.0, -0.5, -1.0, -1.5, -2.0, -3.0, -4.0, -6.0])


def pack_weight(w, fmt):
    k, n = w.shape
    w = f64(bf(w)).reshape(k // 32, 32, n)
    amax = np.abs(w).max(1)
    if fmt == "e4m3":
        byte = np.frexp(amax)[1] - 1 + 127 - 7
    else:
        mant, ex = np.frexp(amax / 6.0)
        byte = np.where(mant > 0.5, ex, ex - 1) + 127
    byte = np.clip(np.where(amax > 0, byte, 1), 1, 254)
    scaled = (w * np.exp2(127.0 - byte)[:, None, :]).reshape(k, n).astype(np.float32)
    by_word = np.ascontiguousarray(scaled.reshape(k // 512, 128, 4, n).transpose(0, 1, 3, 2))
    if fmt == "e4m3":
        words = by_word.astype(ml_dtypes.float8_e4m3fn).view(np.uint8)
    else:
        c = by_word.astype(ml_dtypes.float4_e2m1fn).view(np.uint8) & 0xF
        words = c[..., 0::2] | (c[..., 1::2] << 4)
    return np.ascontiguousarray(words), np.ascontiguousarray(byte.astype(np.uint8).reshape(k // 512, 16, n))


def unpack_weight(words, scales, fmt):
    g, p, n, _ = words.shape
    if fmt == "e4m3":
        vals = np.ascontiguousarray(words).view(ml_dtypes.float8_e4m3fn).astype(np.float64)
    else:
        nib = np.empty((g, p, n, 4), np.uint8)
        nib[..., 0::2] = words & 0xF
        nib[..., 1::2] = words >> 4
        vals = E2M1[nib]
    vals = vals * np.repeat(np.exp2(scales.astype(np.float64) - 127.0), 8, axis=1)[..., None]
    return vals.transpose(0, 1, 3, 2).reshape(g * 512, n)
def pack4(w):
    words, scales = pack_weight(w, "e2m1")
    return words.reshape(words.shape[0], 128, -1), scales


def unpack4(words, scales):
    return unpack_weight(words.reshape(words.shape[0], 128, -1, 2), scales, "e2m1")


E4M3FN = np.array([(-1.0 if i & 128 else 1.0) * ((1.0 + (i & 7) / 8.0) * 2.0 ** (((i >> 3) & 15) - 7) if i & 120 else (i & 7) * 2.0 ** -9) for i in range(256)])


def e4m3fn_bytes(y):
    return np.clip(np.asarray(y, np.float64), -448.0, 448.0).astype(np.float32).astype(ml_dtypes.float8_e4m3fn).view(np.uint8)


def e4m3fn_values(b):
    return E4M3FN[b]


T, J, P, R, Q = 256, 4, 512, 512, 1024


def draw0():
    g, u = mx_kscale(P), mx_kscale(R)
    x = bf(np.random.standard_normal((T, J, P)) * g)
    a = bf(np.random.standard_normal((J, J)) / np.sqrt(J))
    b = bf(np.random.standard_normal((P, R)) / np.sqrt(P) / g[:, None] * u[None, :])
    e = bf(1.0 + 0.1 * np.random.standard_normal(R))
    c_words, c_scales = pack4(np.random.standard_normal((R, Q)) / np.sqrt(R) / u[:, None])
    s = bf(1.0 + 0.1 * np.random.standard_normal(Q))
    return {"x": x,
            "a": a,
            "b": b,
            "e": e,
            "c_words": c_words,
            "c_scales": c_scales,
            "s": s}


def mix_blocks(a, z):
    m = a[:, 0][None, :, None] * z[:, 0, :][:, None, :]
    for j in range(1, a.shape[1]):
        m = m + a[:, j][None, :, None] * z[:, j, :][:, None, :]
    return m


def core(x, a, b, e, c_words, c_scales, s):
    x, a, b, e, s = f64(x), f64(a), f64(b), f64(e), f64(s)
    c = unpack4(c_words, c_scales)
    t, j, p = x.shape
    q = c.shape[1]
    be = b * e[None, :]
    w2 = mxq(be, 1, "e4m3") @ c
    z = (mxq(x.reshape(t * j, p), 1, "e4m3") @ mxq(w2, 0, "e4m3")).reshape(t, j, q)
    m = mix_blocks(a, z)
    return m * s[None, None, :]


def setup_inputs():
    drawn = draw0()
    full = np.asarray(drawn['x']).astype(np.float64)
    scale = (np.abs(full).reshape(256, 4, 4, 128).max(axis=(3,)) / 448.0).astype(np.float32)
    given = {}
    for key, value in drawn.items():
        if key == 'x':
            given['x_bytes'] = e4m3fn_bytes(full / np.repeat(scale.astype(np.float64), 128, axis=2))
            given['x_scale'] = scale
        else:
            given[key] = value
    return given


def reference(x_bytes, x_scale, a, b, e, c_words, c_scales, s):
    return core(e4m3fn_values(x_bytes) * np.repeat(x_scale.astype(np.float64), 128, axis=2), a, b, e, c_words, c_scales, s)

from contextlib import ExitStack

import concourse.mybir as mybir
from concourse.masks import make_identity

F32 = mybir.dt.float32
BF16 = mybir.dt.bfloat16
U32 = mybir.dt.uint32
I32 = mybir.dt.int32
U8 = mybir.dt.uint8
FP8 = mybir.dt.float8_e4m3fn
FP8X4 = mybir.dt.float8_e4m3fn_x4
FP4X4 = mybir.dt.float4_e2m1fn_x4
ALU = mybir.AluOpType
ACT = mybir.ActivationFunctionType
AX = mybir.AxisListType

P = 128
T, J, K, R, Q = 256, 4, 512, 512, 1024
H = 512
FLOPS = 2 * K * R * Q + 2 * T * J * K * Q + 2 * T * J * J * Q


def tile_lokrrankgatedkroneckerdelta_d1p_kernel(tc, x_bytes, x_scale, a, b, e, c_words, c_scales, s, out):
    nc = tc.nc
    with ExitStack() as ctx:
        pool = ctx.enter_context(tc.tile_pool(name="pool", bufs=1))
        psum = ctx.enter_context(tc.psum_pool(name="psum", bufs=1))
        ctx.enter_context(tc.manual_schedule())

        ident = pool.tile([P, P], F32, name="ident", align_bytes=64)
        b_sb = pool.tile([P, 4, R], BF16, name="b_sb", align_bytes=64)
        e_col = pool.tile([P, 4], BF16, name="e_col", align_bytes=64)
        a_row = pool.tile([P, 16], BF16, name="a_row", align_bytes=64)
        a_f = pool.tile([P, 16], F32, name="a_f", align_bytes=64)
        c_sb = pool.tile([P, 2 * Q], U8, name="c_sb", align_bytes=64)
        c_sc = pool.tile([P, Q], U8, name="c_sc", align_bytes=64)
        s_row = pool.tile([P, Q], BF16, name="s_row", align_bytes=64)
        xb = [pool.tile([P, 4, K], U8, name="xb%d" % g, align_bytes=64) for g in range(2)]
        xs = [pool.tile([P, 4, 4], F32, name="xs%d" % g, align_bytes=64) for g in range(2)]
        xv = [pool.tile([P, 4, K], BF16, name="xv%d" % g, align_bytes=64) for g in range(2)]
        xg = [pool.tile([P, 4 * P, 4], BF16, name="xg%d" % g, align_bytes=64) for g in range(2)]
        xq = [pool.tile([P, 4 * P], U32, name="xq%d" % g, align_bytes=64) for g in range(2)]
        xqs = [pool.tile([P, 4 * P], U8, name="xqs%d" % g, align_bytes=64) for g in range(2)]
        bg = pool.tile([P, 4 * P, 4], BF16, name="bg", align_bytes=64)
        bq = pool.tile([P, 4 * P], U32, name="bq", align_bytes=64)
        bqs = pool.tile([P, 4 * P], U8, name="bqs", align_bytes=64)
        wg = pool.tile([P, Q, 4], BF16, name="wg", align_bytes=64)
        wq = pool.tile([P, Q], U32, name="wq", align_bytes=64)
        wqs = pool.tile([P, Q], U8, name="wqs", align_bytes=64)
        EW = 320
        E_COLS = [(0, 512), (512, EW)]
        acc = [pool.tile([P, 4, 512], F32, name="acc%d" % h, align_bytes=64) for h in range(2)]
        prod = pool.tile([P, 8, 512], F32, name="prod", align_bytes=64)
        osb = {}
        zs = {}
        tm = {}
        xg2 = pool.tile([P, 4 * P, 4], BF16, name="xg2", align_bytes=64)
        xq2 = pool.tile([P, 4 * P], U32, name="xq2", align_bytes=64)
        xqs2 = pool.tile([P, 4 * P], U8, name="xqs2", align_bytes=64)
        mask = pool.tile([P, 32], F32, name="mask", align_bytes=64)
        m4 = pool.tile([P, 4], F32, name="m4", align_bytes=64)
        a_sel = pool.tile([P, 4, 4], F32, name="a_sel", align_bytes=64)
        a_col = pool.tile([P, 4], F32, name="a_col", align_bytes=64)
        a_mat = pool.tile([P, 32, 4], F32, name="a_mat", align_bytes=64)

        def bank(tag):
            return psum.tile([P, 512], F32, name=tag)

        nc.vector.memset(c_sc[:].bitcast(I32), 0)
        make_identity(nc, ident[:])
        b_view = b.rearrange("(m t) r -> m t r", t=4)
        for t in range(4):
            nc.sync.dma_start(out=b_sb[:, t, :], in_=b_view[:, t, :])
        nc.scalar.dma_start(out=e_col[:], in_=e.rearrange("(p t) -> p t", t=4))
        nc.scalar.dma_start(out=a_row[:], in_=a.rearrange("i j -> (i j)").partition_broadcast(P))
        x_rows = [x_bytes[128:256], x_bytes[0:128].rearrange("(n u) j k -> (u j) n k", n=4)]
        s_rows = [x_scale[128:256], x_scale[0:128].rearrange("(n u) j k -> (u j) n k", n=4)]
        nc.scalar.dma_start(out=xs[0][:], in_=s_rows[0])
        for q in range(4):
            nc.scalar.dma_start(out=c_sc[32 * q:32 * q + 4, :].bitcast(I32), in_=c_scales[0, 4 * q:4 * q + 4, :].bitcast(I32))
        nc.scalar.dma_start(out=xs[1][:], in_=s_rows[1])
        nc.sync.dma_start(out=xb[0][:], in_=x_rows[0])
        nc.sync.dma_start(out=c_sb[:], in_=c_words[0])
        nc.sync.dma_start(out=xb[1][:], in_=x_rows[1])
        nc.sync.dma_start(out=s_row[:], in_=s.partition_broadcast(P))

        nc.scalar.activation(out=a_f[:], in_=a_row[:], func=ACT.Copy)
        nc.vector.tensor_reduce(out=mask[:], in_=ident[:].rearrange("p (t j) -> p t j", j=4), axis=AX.X, op=ALU.add)
        nc.vector.tensor_reduce(out=m4[:], in_=ident[:].rearrange("p (t j) -> p j t", j=4), axis=AX.X, op=ALU.add)

        def turn(src, slot, dst, half):
            words = src[:, slot, :].bitcast(F32)
            for u in range(2):
                nc.tensor.transpose(dst[:, (2 * half + u) * P:(2 * half + u + 1) * P], words[:, u::2], ident[:])

        def gate(slot, bk):
            src = bk[:].bitcast(BF16)[:, 0:512]
            nc.vector.tensor_tensor(
                out=bg[:, slot * P:(slot + 1) * P, :].rearrange("p r (u w) -> p r u w", w=2),
                in0=src.rearrange("p (u r w) -> p r u w", u=2, w=2),
                in1=e_col[:].rearrange("p (o u w) -> p o u w", o=1, w=2).to_broadcast([P, P, 2, 2]),
                op=ALU.mult)

        def quant(codes, planes, src, lo, hi):
            nc.vector.quantize_mx(
                out=codes[:, lo:hi].bitcast(FP8X4), scales=planes[:, lo:hi],
                in_=src[:, lo:hi, :].rearrange("p r t -> p (r t)"))

        def widen(g, slot, blk, on_vector):
            cols = slice(blk * P, (blk + 1) * P)
            src = xb[g][:, slot, cols].bitcast(FP8)
            if on_vector:
                nc.vector.tensor_scalar(out=xv[g][:, slot, cols], in0=src, scalar1=xs[g][:, slot, blk:blk + 1], scalar2=None, op0=ALU.mult)
            else:
                nc.scalar.activation(out=xv[g][:, slot, cols], in_=src, func=ACT.Copy, scale=xs[g][:, slot, blk:blk + 1])

        def gather_words(g, pair, bk, on_vector):
            (nc.vector.tensor_copy if on_vector else nc.scalar.copy)(
                out=xg[g][:, pair * 256:(pair + 1) * 256, :].rearrange("p r t -> p (r t)").bitcast(F32).rearrange("p (s r u) -> p s r u", s=2, u=2),
                in_=bk[:].rearrange("p (s u r) -> p s r u", s=2, u=2))

        def factor(qb, bk):
            for t in range(4):
                nc.tensor.matmul_mx(
                    out=bk[:, t * P:(t + 1) * P],
                    lhsT=bq[:, t * P:(t + 1) * P].bitcast(FP8X4), lhsT_scale=bqs[:, t * P:(t + 1) * P],
                    rhs=c_sb[:, 256 * qb:256 * (qb + 1)].bitcast(FP4X4), rhs_scale=c_sc[:, P * qb:P * (qb + 1)],
                    start=True, stop=True)

        def weave(qb, bk, on_vector):
            dst = wg[:, qb * P:(qb + 1) * P, :]
            src = bk[:].rearrange("p (t n) -> p n t", t=4)
            if on_vector:
                nc.vector.tensor_copy(out=dst, in_=src)
            else:
                nc.scalar.copy(out=dst, in_=src)

        def apply(g, slot, h, bk):
            nc.tensor.matmul_mx(
                out=bk[:],
                lhsT=xq[g][:, slot * P:(slot + 1) * P].bitcast(FP8X4), lhsT_scale=xqs[g][:, slot * P:(slot + 1) * P],
                rhs=wq[:, h * H:(h + 1) * H].bitcast(FP8X4), rhs_scale=wqs[:, h * H:(h + 1) * H],
                start=True, stop=True)

        def mix_matrix_a():
            nc.vector.tensor_tensor(out=a_sel[:], in0=a_row[:].rearrange("p (i j) -> p i j", j=4), in1=m4[:].rearrange("p (o j) -> p o j", o=1).to_broadcast([P, 4, 4]), op=ALU.mult)

        def mix_matrix_b():
            nc.vector.tensor_reduce(out=a_col[:], in_=a_sel[:], axis=AX.X, op=ALU.add)

        def mix_matrix_c():
            nc.vector.tensor_tensor(
                out=a_mat[:],
                in0=mask[:].rearrange("p (t o) -> p t o", o=1).to_broadcast([P, 32, 4]),
                in1=a_col[:].rearrange("p (o i) -> p o i", o=1).to_broadcast([P, 32, 4]), op=ALU.mult)

        def reorder():
            nc.gpsimd.tensor_copy(out=xg2[:].rearrange("p (t j) w -> p t j w", j=4), in_=xg[0][:].rearrange("p (j t) w -> p t j w", j=4))

        def quant_reordered():
            quant(xq2, xqs2, xg2, 0, 512)

        def mix_first(h, i, bk):
            n = E_COLS[h][1]
            nc.scalar.activation(out=acc[h][:, i, 0:n], in_=bk[:, 0:n], func=ACT.Copy, scale=a_f[:, 4 * i:4 * i + 1])

        def mix_term(h, i, j, bk):
            n = E_COLS[h][1]
            nc.vector.scalar_tensor_tensor(out=acc[h][:, i, 0:n], in0=bk[:, 0:n], scalar=a_f[:, 4 * i + j:4 * i + j + 1], in1=acc[h][:, i, 0:n], op0=ALU.mult, op1=ALU.add)

        def mix_last(h, i, bk):
            n = E_COLS[h][1]
            nc.scalar.activation(out=prod[:, 4 * h + i, 0:n], in_=bk[:, 0:n], func=ACT.Copy, scale=a_f[:, 4 * i + 3:4 * i + 4])

        def mix_add(h, i):
            n = E_COLS[h][1]
            nc.gpsimd.tensor_tensor(out=acc[h][:, i, 0:n], in0=acc[h][:, i, 0:n], in1=prod[:, 4 * h + i, 0:n], op=ALU.add)

        def mix_end(h, i):
            q0, n = E_COLS[h]
            o = pool.tile([P, n], F32, name="oe%d_%d" % (h, i), align_bytes=64)
            nc.gpsimd.tensor_tensor(out=o[:], in0=acc[h][:, i, 0:n], in1=s_row[:, q0:q0 + n], op=ALU.mult)
            nc.sync.dma_start(out=out[128:256][:, i, q0:q0 + n], in_=o[:])

        out_rows = [out[128 * g:128 * (g + 1)].rearrange("(n u) i q -> (u i) n q", n=4) for g in range(2)]
        REST = 512 - EW

        def unit_z(k, bk):
            if k < 8:
                apply(1, k % 4, k // 4, bk)
            else:
                for r in range(2):
                    n = 2 * (k - 8) + r
                    nc.tensor.matmul_mx(
                        out=bk[:, 256 * r:256 * r + 256],
                        lhsT=xq2[:, n * P:(n + 1) * P].bitcast(FP8X4), lhsT_scale=xqs2[:, n * P:(n + 1) * P],
                        rhs=wq[:, 768:1024].bitcast(FP8X4), rhs_scale=wqs[:, 768:1024],
                        start=True, stop=True)

        def unit_copy(k, bk):
            if k < 8:
                t = pool.tile([P, 512], F32, name="zs%d" % k, align_bytes=64)
                nc.scalar.copy(out=t[:], in_=bk[:])
            else:
                t = pool.tile([P, 2 * REST], F32, name="zs%d" % k, align_bytes=64)
                nc.scalar.copy(out=t[:].rearrange("p (r q) -> p r q", r=2), in_=bk[:].rearrange("p (r q) -> p r q", r=2)[:, :, 256 - REST:256])
            zs[k] = t

        def unit_mix(k, bk):
            n = 512 if k < 8 else 2 * REST
            nc.tensor.matmul(bk[:, 0:n], lhsT=a_mat[:].rearrange("p t i -> p (t i)"), rhs=zs[k][:], start=True, stop=True)

        def scale_of(k):
            if k < 8:
                h = k // 4
                return s_row[:, h * H:(h + 1) * H]
            return s_row[:, Q - REST:Q].rearrange("p (o q) -> p o q", o=1).to_broadcast([P, 2, REST])

        def unit_view(k, t):
            n = 512 if k < 8 else 2 * REST
            return t[:, 0:n] if k < 8 else t[:, 0:n].rearrange("p (r q) -> p r q", r=2)

        def unit_store(k, o):
            if k < 8:
                nc.sync.dma_start(out=out_rows[0][:, k % 4, (k // 4) * H:(k // 4 + 1) * H], in_=o[:])
            else:
                nc.sync.dma_start(out=out_rows[1][:, 2 * (k - 8):2 * (k - 8) + 2, Q - REST:Q], in_=unit_view(k, o))

        def unit_out(k, bk):
            n = 512 if k < 8 else 2 * REST
            t = pool.tile([P, n], F32, name="tm%d" % k, align_bytes=64)
            nc.scalar.copy(out=t[:], in_=bk[:, 0:n])
            tm[k] = t

        def unit_scale(k):
            n = 512 if k < 8 else 2 * REST
            o = pool.tile([P, n], F32, name="om%d" % k, align_bytes=64)
            nc.gpsimd.tensor_tensor(out=unit_view(k, o), in0=unit_view(k, tm[k]), in1=scale_of(k), op=ALU.mult)
            unit_store(k, o)

        def unit_end(k, bk):
            n = 512 if k < 8 else 2 * REST
            o = pool.tile([P, n], F32, name="om%d" % k, align_bytes=64)
            nc.vector.tensor_tensor(out=unit_view(k, o), in0=unit_view(k, bk), in1=scale_of(k), op=ALU.mult)
            unit_store(k, o)

        B = {}
        mix_matrix_a()
        B["b0"] = bank("e0")
        turn(b_sb, 0, B["b0"], 0)
        mix_matrix_b()
        B["b1"] = bank("e1")
        turn(b_sb, 1, B["b1"], 0)
        mix_matrix_c()
        B["b2"] = bank("e2")
        turn(b_sb, 2, B["b2"], 0)
        gate(0, B["b0"])
        B["b3"] = bank("e3")
        turn(b_sb, 3, B["b3"], 0)
        gate(1, B["b1"])
        widen(0, 1, 0, False)
        widen(0, 1, 1, False)
        widen(0, 1, 2, False)
        widen(0, 1, 3, False)
        gate(2, B["b2"])
        widen(0, 0, 0, False)
        widen(0, 0, 1, False)
        widen(0, 0, 2, False)
        widen(0, 0, 3, False)
        gate(3, B["b3"])
        B["x00"] = bank("m0")
        turn(xv[0], 1, B["x00"], 1)
        widen(1, 0, 0, True)
        widen(1, 0, 1, True)
        widen(1, 0, 2, True)
        widen(1, 0, 3, True)
        widen(1, 1, 0, False)
        widen(1, 1, 1, False)
        widen(1, 1, 2, False)
        widen(1, 1, 3, False)
        turn(xv[0], 0, B["x00"], 0)
        quant(bq, bqs, bg, 256, 512)
        widen(1, 2, 0, False)
        widen(1, 2, 1, False)
        widen(1, 2, 2, False)
        widen(1, 2, 3, False)
        quant(bq, bqs, bg, 0, 256)
        widen(1, 3, 0, True)
        widen(1, 3, 1, True)
        widen(1, 3, 2, True)
        widen(1, 3, 3, True)
        B["w5"] = bank("z1")
        factor(5, B["w5"])
        gather_words(0, 0, B["x00"], False)
        widen(0, 3, 0, True)
        widen(0, 3, 1, True)
        widen(0, 3, 2, True)
        widen(0, 3, 3, True)
        B["w2"] = bank("e2")
        factor(2, B["w2"])
        B["w1"] = bank("e1")
        factor(1, B["w1"])
        weave(5, B["w5"], False)
        B["w3"] = bank("e3")
        factor(3, B["w3"])
        quant(xq[0], xqs[0], xg[0], 0, 256)
        B["w4"] = bank("z0")
        factor(4, B["w4"])
        weave(2, B["w2"], True)
        widen(0, 2, 0, False)
        widen(0, 2, 1, False)
        widen(0, 2, 2, False)
        widen(0, 2, 3, False)
        B["w0"] = bank("e0")
        factor(0, B["w0"])
        B["x11"] = bank("z1")
        turn(xv[1], 2, B["x11"], 0)
        weave(1, B["w1"], True)
        weave(3, B["w3"], False)
        turn(xv[1], 3, B["x11"], 1)
        B["x01"] = bank("m1")
        turn(xv[0], 2, B["x01"], 0)
        weave(0, B["w0"], True)
        turn(xv[0], 3, B["x01"], 1)
        weave(4, B["w4"], False)
        B["w6"] = bank("m0")
        factor(6, B["w6"])
        quant(wq, wqs, wg, 256, 512)
        gather_words(1, 1, B["x11"], False)
        quant(wq, wqs, wg, 0, 256)
        B["x10"] = bank("z0")
        turn(xv[1], 1, B["x10"], 1)
        quant(wq, wqs, wg, 512, 768)
        turn(xv[1], 0, B["x10"], 0)
        gather_words(0, 1, B["x01"], False)
        weave(6, B["w6"], True)
        B["E01"] = bank("e1")
        apply(0, 1, 0, B["E01"])
        B["E00"] = bank("e0")
        apply(0, 0, 0, B["E00"])
        gather_words(1, 0, B["x10"], False)
        quant(xq[1], xqs[1], xg[1], 256, 512)
        B["w7"] = bank("m1")
        factor(7, B["w7"])
        reorder()
        quant(xq[0], xqs[0], xg[0], 256, 512)
        mix_first(0, 2, B["E00"])
        quant(xq[1], xqs[1], xg[1], 0, 256)
        B["z2"] = bank("z0")
        unit_z(2, B["z2"])
        B["E03"] = bank("e3")
        apply(0, 3, 0, B["E03"])
        weave(7, B["w7"], True)
        mix_first(0, 0, B["E00"])
        B["E02"] = bank("e2")
        apply(0, 2, 0, B["E02"])
        mix_term(0, 2, 1, B["E01"])
        mix_first(0, 1, B["E00"])
        quant(wq, wqs, wg, 768, 1024)
        unit_copy(2, B["z2"])
        mix_term(0, 2, 2, B["E02"])
        B["z4"] = bank("z1")
        unit_z(4, B["z4"])
        mix_last(0, 2, B["E03"])
        B["m2"] = bank("m0")
        unit_mix(2, B["m2"])
        quant_reordered()
        unit_copy(4, B["z4"])
        mix_add(0, 2)
        mix_term(0, 0, 1, B["E01"])
        mix_first(0, 3, B["E00"])
        B["z0"] = bank("z0")
        unit_z(0, B["z0"])
        mix_term(0, 1, 1, B["E01"])
        B["m4"] = bank("m1")
        unit_mix(4, B["m4"])
        unit_out(2, B["m2"])
        mix_term(0, 0, 2, B["E02"])
        mix_end(0, 2)
        unit_copy(0, B["z0"])
        mix_term(0, 1, 2, B["E02"])
        B["E10"] = bank("e0")
        apply(0, 0, 1, B["E10"])
        B["z6"] = bank("z1")
        unit_z(6, B["z6"])
        mix_term(0, 0, 3, B["E03"])
        B["z5"] = bank("z0")
        unit_z(5, B["z5"])
        mix_first(1, 2, B["E10"])
        B["m0"] = bank("m0")
        unit_mix(0, B["m0"])
        unit_scale(2)
        unit_copy(6, B["z6"])
        unit_end(4, B["m4"])
        mix_first(1, 1, B["E10"])
        mix_term(0, 1, 3, B["E03"])
        B["m6"] = bank("m1")
        unit_mix(6, B["m6"])
        mix_first(1, 3, B["E10"])
        mix_end(0, 0)
        mix_term(0, 3, 1, B["E01"])
        mix_first(1, 0, B["E10"])
        unit_copy(5, B["z5"])
        unit_end(0, B["m0"])
        B["z8"] = bank("z1")
        unit_z(8, B["z8"])
        B["E11"] = bank("e1")
        apply(0, 1, 1, B["E11"])
        mix_term(0, 3, 2, B["E02"])
        mix_end(0, 1)
        unit_out(6, B["m6"])
        B["z9"] = bank("z0")
        unit_z(9, B["z9"])
        B["m5"] = bank("m0")
        unit_mix(5, B["m5"])
        mix_term(1, 0, 1, B["E11"])
        unit_copy(8, B["z8"])
        mix_term(0, 3, 3, B["E03"])
        unit_copy(9, B["z9"])
        unit_scale(6)
        B["m8"] = bank("m1")
        unit_mix(8, B["m8"])
        mix_term(1, 3, 1, B["E11"])
        mix_term(1, 2, 1, B["E11"])
        unit_end(5, B["m5"])
        B["E12"] = bank("e2")
        apply(0, 2, 1, B["E12"])
        B["E13"] = bank("e3")
        apply(0, 3, 1, B["E13"])
        mix_end(0, 3)
        B["z7"] = bank("z1")
        unit_z(7, B["z7"])
        unit_end(8, B["m8"])
        B["z3"] = bank("z0")
        unit_z(3, B["z3"])
        mix_last(1, 3, B["E13"])
        B["m9"] = bank("m0")
        unit_mix(9, B["m9"])
        mix_term(1, 3, 2, B["E12"])
        unit_copy(7, B["z7"])
        mix_term(1, 0, 2, B["E12"])
        mix_add(1, 3)
        mix_term(1, 2, 2, B["E12"])
        unit_copy(3, B["z3"])
        B["m7"] = bank("m1")
        unit_mix(7, B["m7"])
        mix_term(1, 0, 3, B["E13"])
        mix_term(1, 2, 3, B["E13"])
        mix_end(1, 3)
        unit_end(9, B["m9"])
        B["z1"] = bank("z1")
        unit_z(1, B["z1"])
        mix_term(1, 1, 1, B["E11"])
        mix_end(1, 2)
        B["m3"] = bank("m0")
        unit_mix(3, B["m3"])
        unit_end(7, B["m7"])
        unit_copy(1, B["z1"])
        mix_term(1, 1, 2, B["E12"])
        mix_end(1, 0)
        B["m1"] = bank("m1")
        unit_mix(1, B["m1"])
        mix_term(1, 1, 3, B["E13"])
        unit_end(3, B["m3"])
        mix_end(1, 1)
        unit_end(1, B["m1"])
